import numpy as np
import ml_dtypes


def mxq(x, axis, fmt="e4m3"):
    dtype, down = {"e4m3": (ml_dtypes.float8_e4m3fn, 7), "e5m2": (ml_dtypes.float8_e5m2, 14)}[fmt]
    v = np.moveaxis(np.asarray(x, np.float32).astype(ml_dtypes.bfloat16).astype(np.float64), axis, -1)
    blocks = v.reshape(v.shape[:-1] + (-1, 32))
    amax = np.abs(blocks).max(-1, keepdims=True)
    byte = np.maximum(np.where(amax > 0, np.frexp(amax)[1] - 1 + 127, 0) - down, 1)
    scale = np.exp2(byte - 127.0)
    codes = (blocks / scale).astype(np.float32).astype(dtype).astype(np.float64)
    return np.moveaxis((codes * scale).reshape(v.shape), -1, axis)


WIDE = False


def mx_kscale(k):
    if not WIDE:
        return np.ones(k)
    levels = np.array([10, -10, 5, -5, 0])
    if k % 512:
        return np.exp2(np.random.permutation(np.resize(levels, k // 32))).repeat(32)
    a = np.empty((k // 512, 16))
    for p in range(k // 512):
        a[p, :8] = np.random.permutation(np.resize(levels, 8))
        for g in range(8):
            far = levels[np.abs(levels - a[p, g]) >= 10]
            a[p, g + 8] = far[np.random.randint(len(far))]
    return np.exp2(a.ravel()).repeat(32)


def f64(x):
    return np.asarray(x).astype(np.float64)


def striped(idx):
    return np.tile(np.asarray(idx).reshape(-1, 16).T, (8, 1)).astype(np.uint16)


def unstriped(offs):
    return offs[:16].T.reshape(-1).astype(np.int64)


E2M1 = np.array([0.0, 0.5, 1.0, 1.5, 2.0, 3.0, 4.0, 6.0, -0.0, -0.5, -1.0, -1.5, -2.0, -3.0, -4.0, -6.0])


def pack_weight(w, fmt):
    k, n = w.shape
    w = f64(np.asarray(w, np.float32).astype(ml_dtypes.bfloat16)).reshape(k // 32, 32, n)
    amax = np.abs(w).max(1)
    if fmt == "e4m3":
        byte = np.frexp(amax)[1] - 1 + 127 - 7
    else:
        mant, ex = np.frexp(amax / 6.0)
        byte = np.where(mant > 0.5, ex, ex - 1) + 127
    byte = np.clip(np.where(amax > 0, byte, 1), 1, 254)
    scaled = (w * np.exp2(127.0 - byte)[:, None, :]).reshape(k, n).astype(np.float32)
    by_word = np.ascontiguousarray(scaled.reshape(k // 512, 128, 4, n).transpose(0, 1, 3, 2))
    if fmt == "e4m3":
        words = by_word.astype(ml_dtypes.float8_e4m3fn).view(np.uint8)
    else:
        c = by_word.astype(ml_dtypes.float4_e2m1fn).view(np.uint8) & 0xF
        words = (c[..., 0::2] | (c[..., 1::2] << 4)).reshape(k // 512, 128, 2 * n)
    return np.ascontiguousarray(words), np.ascontiguousarray(byte.astype(np.uint8).reshape(k // 512, 16, n))


def unpack_weight(words, scales, fmt):
    g, _, n = scales.shape
    words = np.ascontiguousarray(words).reshape(g, 128, n, -1)
    if fmt == "e4m3":
        vals = words.view(ml_dtypes.float8_e4m3fn).astype(np.float64)
    else:
        nib = np.empty((g, 128, n, 4), np.uint8)
        nib[..., 0::2] = words & 0xF
        nib[..., 1::2] = words >> 4
        vals = E2M1[nib]
    vals = vals * np.repeat(np.exp2(scales.astype(np.float64) - 127.0), 8, axis=1)[..., None]
    return vals.transpose(0, 1, 3, 2).reshape(g * 512, n)


D, T, I, Q, J, U, M = 512, 2048, 512, 128, 512, 1024, 2048


def setup_inputs():
    n = np.random.standard_normal
    idx = np.random.permutation(T)[:I]
    idx2 = np.random.permutation(U)[:J]
    idx3 = np.random.permutation(M)[:I]
    fd = mx_kscale(D)
    fj = mx_kscale(J)
    tiesp = pack_weight(n((J, T)) * 0.08 / fj[:, None], "e2m1")
    return {
        "query": (n((D, Q)) * 1.0 / np.sqrt(D) * fd[:, None]).astype(np.float32),
        "hubs": (n((D, U)) / fd[:, None]).astype(np.float32),
        "hf": (np.random.uniform(0.5, 2.0, (J, 1)) * fj[:, None]).astype(np.float32),
        "ties_words": tiesp[0],
        "ties_scales": tiesp[1],
        "old": (np.random.uniform(0.0, 2.0, (Q, M))).astype(np.float32),
        "fade": (np.random.uniform(0.3, 0.9, (Q, 1))).astype(np.float32),
        "offs": striped(idx),
        "offs2": striped(idx2),
        "offs3": striped(idx3),
    }


def reference(query, hubs, hf, ties_words, ties_scales, old, fade, offs, offs2, offs3):
    idx = unstriped(offs)
    idx2 = unstriped(offs2)
    idx3 = unstriped(offs3)
    tiesu = unpack_weight(ties_words, ties_scales, "e2m1")
    hubsidx2q = mxq(f64(hubs)[:, idx2], 0, "e4m3")
    queryq = mxq(f64(query), 0, "e4m3")
    hb = hubsidx2q.T @ queryq
    hp = np.maximum(hb, 0.0) * f64(hf)
    hpq = mxq(hp, 0, "e4m3")
    tiesidxg = tiesu[:, idx]
    s = hpq.T @ tiesidxg
    w = np.maximum(s, 0.0)
    ws = w * 2.0
    wf = np.zeros((Q, M))
    wf[:, idx3] = ws
    y = f64(old) * f64(fade) + wf
    return y

@@ -1,0 +1,189 @@
+from contextlib import ExitStack
+
+import concourse.mybir as mybir
+
+D, T, I, Q, J, U, M = 512, 2048, 512, 128, 512, 1024, 2048
+FLOPS = 2 * J * D * Q + 2 * Q * J * I
+
+F32 = mybir.dt.float32
+BF16 = mybir.dt.bfloat16
+I32 = mybir.dt.int32
+U32 = mybir.dt.uint32
+U16 = mybir.dt.uint16
+U8 = mybir.dt.uint8
+FP8X4 = mybir.dt.float8_e4m3fn_x4
+FP4X4 = mybir.dt.float4_e2m1fn_x4
+ALU = mybir.AluOpType
+ACT = mybir.ActivationFunctionType
+
+P = 128
+PACK = 4
+HALF = 256
+LIST_COLS = HALF // 16
+OUT_EDGES = (0, 256, 768, 1280, 1792, 2048)
+
+
+def tile_attend_relayed_counts_lean_kernel(
+    tc, query, hubs, hf, ties_words, ties_scales, old, fade, offs, offs2, offs3, out
+):
+    nc = tc.nc
+    with ExitStack() as ctx:
+        sb = ctx.enter_context(tc.tile_pool(name="sb", bufs=1))
+        ps = ctx.enter_context(tc.psum_pool(name="ps", bufs=1))
+
+        def half_of(lst, h):
+            return lst[:, h * LIST_COLS : (h + 1) * LIST_COLS]
+
+        tie_list = sb.tile([P, I // 16], U16, name="tie_list")
+        hub_list = sb.tile([P, J // 16], U16, name="hub_list")
+        col_list = sb.tile([P, I // 16], U16, name="col_list")
+
+        tie_scales = sb.tile([P, T], U8, name="tie_scales", align_bytes=64)
+        nc.vector.memset(tie_scales[:].bitcast(I32), 0)
+        placed = sb.tile([P, M], F32, name="placed")
+        nc.vector.memset(placed[:], 0.0)
+
+        nc.sync.dma_start(hub_list[:], offs2)
+        q_raw = sb.tile([P, PACK, Q], F32, name="q_raw")
+        nc.sync.dma_start(q_raw[:], query.rearrange("(p t) q -> p t q", t=PACK))
+        hub_rows = hubs.rearrange("(p t) u -> t p u", t=PACK)
+        planes = [sb.tile([P, U], F32, name="plane%d" % t) for t in range(PACK)]
+        for k in range(4):
+            nc.sync.dma_start(
+                tie_scales[k:P:32, :].bitcast(I32), ties_scales[0, k:16:4, :].bitcast(I32)
+            )
+        nc.sync.dma_start(tie_list[:], offs)
+        for t in range(PACK):
+            nc.sync.dma_start(planes[t][:], hub_rows[t])
+        tie_words = sb.tile([P, T], U16, name="tie_words", align_bytes=64)
+        nc.sync.dma_start(tie_words[:].bitcast(I32), ties_words[0].bitcast(I32))
+        hf_sb = sb.tile([P, PACK], F32, name="hf_sb", tag="words1", align_bytes=64)
+        nc.sync.dma_start(hf_sb[:], hf.rearrange("(p t) o -> p (t o)", t=PACK))
+        nc.sync.dma_start(col_list[:], offs3)
+        old_sb = sb.tile([P, M], F32, name="old_sb")
+        nc.sync.dma_start(old_sb[:], old)
+        fade_sb = sb.tile([P, 1], F32, name="fade_sb")
+        nc.sync.dma_start(fade_sb[:], fade)
+
+        q_bf = sb.tile([P, Q, PACK], BF16, name="q_bf", align_bytes=64)
+        nc.scalar.activation(
+            q_bf[:].rearrange("p (c i) t -> p c t i", i=4),
+            q_raw[:].rearrange("p t (c i) -> p c t i", i=4),
+            ACT.Copy,
+        )
+        q_codes = sb.tile([P, Q], U32, name="q_codes", align_bytes=64)
+        q_scales = sb.tile([P, Q], U8, name="q_scales", align_bytes=64)
+        nc.vector.quantize_mx(
+            out=q_codes[:].bitcast(FP8X4),
+            scales=q_scales[:],
+            in_=q_bf[:].rearrange("p q t -> p (q t)"),
+        )
+
+        S = HALF // PACK
+        dealt0 = sb.tile([P, PACK, S, PACK], BF16, name="dealt0", align_bytes=64)
+        picked = sb.tile([P, PACK, HALF], BF16, name="picked", tag="words0", align_bytes=64)
+        slot_scales = sb.tile([P, I], U8, name="slot_scales", align_bytes=64)
+        for t in range(PACK):
+            nc.vector.tensor_copy(
+                dealt0[:].rearrange("p r s t -> p s r t")[:, :, :, t],
+                planes[t][:].indirect(half_of(hub_list, 0)),
+            )
+            nc.scalar.activation(
+                picked[:, t, :], planes[t][:].indirect(half_of(hub_list, 1)), ACT.Copy
+            )
+            if t < 2:
+                nc.vector.tensor_copy(
+                    slot_scales[:, t * HALF : (t + 1) * HALF],
+                    tie_scales[:].indirect(half_of(tie_list, t)),
+                )
+
+        hub_codes = sb.tile([P, PACK, P], U32, name="hub_codes", align_bytes=64)
+        hub_scales = sb.tile([P, PACK, P], U8, name="hub_scales", align_bytes=64)
+
+        def quantize_hubs(dealt, h, r0):
+            for r in range(dealt.shape[1]):
+                cols = slice(h * S, (h + 1) * S)
+                nc.vector.quantize_mx(
+                    out=hub_codes[:, r0 + r, cols].bitcast(FP8X4),
+                    scales=hub_scales[:, r0 + r, cols],
+                    in_=dealt[:, r, :, :].rearrange("p s t -> p (s t)"),
+                )
+
+        dealt1 = [sb.tile([P, 2, S, PACK], BF16, name="dealt1_%d" % c, align_bytes=64) for c in range(2)]
+        picked_str = picked[:].rearrange("p t (s r) -> p s t r", r=PACK)
+        nc.scalar.copy(dealt1[1][:].rearrange("p r s t -> p s t r"), picked_str[:, :, :, 2:4])
+        quantize_hubs(dealt0, 0, 0)
+        nc.vector.tensor_copy(dealt1[0][:].rearrange("p r s t -> p s t r"), picked_str[:, :, :, 0:2])
+        for c in range(2):
+            quantize_hubs(dealt1[c], 1, 2 * c)
+
+        hb = ps.tile([P, PACK, Q], F32, name="hb")
+        for r in range(PACK):
+            nc.tensor.matmul_mx(
+                out=hb[:, r, :],
+                lhsT=hub_codes[:, r, :].bitcast(FP8X4),
+                lhsT_scale=hub_scales[:, r, :],
+                rhs=q_codes[:].bitcast(FP8X4),
+                rhs_scale=q_scales[:],
+                start=True,
+                stop=True,
+            )
+
+        QH = Q // 2
+        hp_bf = [sb.tile([P, QH, PACK], BF16, name="hp_bf%d" % h, align_bytes=64) for h in range(2)]
+        hp_codes = sb.tile([P, Q], U32, name="hp_codes", align_bytes=64)
+        hp_scales = sb.tile([P, Q], U8, name="hp_scales", align_bytes=64)
+        for h in range(2):
+            nc.vector.scalar_tensor_tensor(
+                out=hp_bf[h][:],
+                in0=hb[:].rearrange("p r q -> p q r")[:, h * QH : (h + 1) * QH, :],
+                scalar=0.0,
+                in1=hf_sb[:].unsqueeze(1).to_broadcast([P, QH, PACK]),
+                op0=ALU.max,
+                op1=ALU.mult,
+            )
+        for h in range(2):
+            nc.vector.quantize_mx(
+                out=hp_codes[:, h * QH : (h + 1) * QH].bitcast(FP8X4),
+                scales=hp_scales[:, h * QH : (h + 1) * QH],
+                in_=hp_bf[h][:].rearrange("p q t -> p (q t)"),
+            )
+
+        slot_words = [sb.tile([P, HALF], U16, name="slot_words%d" % h, tag="words%d" % h, align_bytes=64) for h in range(2)]
+        for h in range(2):
+            nc.vector.tensor_copy(slot_words[h][:], tie_words[:].indirect(half_of(tie_list, h)))
+        FIRST = 128
+        w_first = sb.tile([P, FIRST], F32, name="w_first")
+        ws_rest = sb.tile([P, I - FIRST], F32, name="ws_rest")
+        for lo, hi in ((0, FIRST), (FIRST, HALF), (HALF, I)):
+            h = lo // HALF
+            score = ps.tile([P, hi - lo], F32, name="score%d" % lo)
+            nc.tensor.matmul_mx(
+                out=score[:],
+                lhsT=hp_codes[:].bitcast(FP8X4),
+                lhsT_scale=hp_scales[:],
+                rhs=slot_words[h][:, lo - h * HALF : hi - h * HALF].bitcast(FP4X4),
+                rhs_scale=slot_scales[:, lo:hi],
+                start=True,
+                stop=True,
+            )
+            if lo == 0:
+                nc.scalar.activation(w_first[:], score[:], ACT.Relu)
+            else:
+                nc.scalar.activation(ws_rest[:, lo - FIRST : hi - FIRST], score[:], ACT.Relu, scale=2.0)
+        nc.vector.tensor_tensor(
+            placed[:].indirect(col_list[:, : FIRST // 16]), w_first[:], w_first[:], ALU.add
+        )
+        nc.vector.tensor_copy(placed[:].indirect(col_list[:, FIRST // 16 :]), ws_rest[:])
+
+        for lo, hi in zip(OUT_EDGES[:-1], OUT_EDGES[1:]):
+            res = sb.tile([P, hi - lo], F32, name="res%d" % lo)
+            nc.vector.scalar_tensor_tensor(
+                out=res[:],
+                in0=old_sb[:, lo:hi],
+                scalar=fade_sb[:],
+                in1=placed[:, lo:hi],
+                op0=ALU.mult,
+                op1=ALU.add,
+            )
+            nc.sync.dma_start(out[:, lo:hi], res[:])

@@ -38,30 +38,26 @@ def tile_attend_relayed_counts_lean_kernel(
         hub_list = sb.tile([P, J // 16], U16, name="hub_list")
         col_list = sb.tile([P, I // 16], U16, name="col_list")
 
-        tie_scales = sb.tile([P, T], U8, name="tie_scales", align_bytes=64)
+        tie_scales = sb.tile([P, T], U8, name="tie_scales", tag="old", align_bytes=64)
         nc.vector.memset(tie_scales[:].bitcast(I32), 0)
         placed = sb.tile([P, M], F32, name="placed")
         nc.vector.memset(placed[:], 0.0)
 
         nc.sync.dma_start(hub_list[:], offs2)
-        q_raw = sb.tile([P, PACK, Q], F32, name="q_raw")
-        nc.sync.dma_start(q_raw[:], query.rearrange("(p t) q -> p t q", t=PACK))
         hub_rows = hubs.rearrange("(p t) u -> t p u", t=PACK)
         planes = [sb.tile([P, U], F32, name="plane%d" % t) for t in range(PACK)]
-        for k in range(4):
-            nc.sync.dma_start(
-                tie_scales[k:P:32, :].bitcast(I32), ties_scales[0, k:16:4, :].bitcast(I32)
-            )
+        nc.sync.dma_start(planes[0][:], hub_rows[0])
         nc.sync.dma_start(tie_list[:], offs)
-        for t in range(PACK):
+        nc.sync.dma_start(tie_scales[0:P:8, :].bitcast(I32), ties_scales[0].bitcast(I32))
+        q_raw = sb.tile([P, PACK, Q], F32, name="q_raw", tag="words0", align_bytes=64)
+        nc.sync.dma_start(q_raw[:], query.rearrange("(p t) q -> p t q", t=PACK))
+        for t in range(1, PACK):
             nc.sync.dma_start(planes[t][:], hub_rows[t])
         tie_words = sb.tile([P, T], U16, name="tie_words", align_bytes=64)
         nc.sync.dma_start(tie_words[:].bitcast(I32), ties_words[0].bitcast(I32))
         hf_sb = sb.tile([P, PACK], F32, name="hf_sb", tag="words1", align_bytes=64)
         nc.sync.dma_start(hf_sb[:], hf.rearrange("(p t) o -> p (t o)", t=PACK))
         nc.sync.dma_start(col_list[:], offs3)
-        old_sb = sb.tile([P, M], F32, name="old_sb")
-        nc.sync.dma_start(old_sb[:], old)
         fade_sb = sb.tile([P, 1], F32, name="fade_sb")
         nc.sync.dma_start(fade_sb[:], fade)
 
@@ -82,7 +78,7 @@ def tile_attend_relayed_counts_lean_kernel(
         S = HALF // PACK
         dealt0 = sb.tile([P, PACK, S, PACK], BF16, name="dealt0", align_bytes=64)
         picked = sb.tile([P, PACK, HALF], BF16, name="picked", tag="words0", align_bytes=64)
-        slot_scales = sb.tile([P, I], U8, name="slot_scales", align_bytes=64)
+        spread_scales = sb.tile([P, I], U8, name="spread_scales")
         for t in range(PACK):
             nc.vector.tensor_copy(
                 dealt0[:].rearrange("p r s t -> p s r t")[:, :, :, t],
@@ -93,9 +89,17 @@ def tile_attend_relayed_counts_lean_kernel(
             )
             if t < 2:
                 nc.vector.tensor_copy(
-                    slot_scales[:, t * HALF : (t + 1) * HALF],
+                    spread_scales[:, t * HALF : (t + 1) * HALF],
                     tie_scales[:].indirect(half_of(tie_list, t)),
                 )
+        slot_scales = sb.tile([P, I], U8, name="slot_scales", align_bytes=64)
+        nc.vector.memset(slot_scales[:].bitcast(I32), 0)
+        for k in range(4):
+            nc.sync.dma_start(
+                slot_scales[k:P:32, :].bitcast(I32), spread_scales[8 * k : P : 32, :].bitcast(I32)
+            )
+        old_sb = sb.tile([P, M], F32, name="old_sb", tag="old", align_bytes=64)
+        nc.sync.dma_start(old_sb[:], old)
 
         hub_codes = sb.tile([P, PACK, P], U32, name="hub_codes", align_bytes=64)
         hub_scales = sb.tile([P, PACK, P], U8, name="hub_scales", align_bytes=64)
@@ -112,8 +116,8 @@ def tile_attend_relayed_counts_lean_kernel(
         dealt1 = [sb.tile([P, 2, S, PACK], BF16, name="dealt1_%d" % c, align_bytes=64) for c in range(2)]
         picked_str = picked[:].rearrange("p t (s r) -> p s t r", r=PACK)
         nc.scalar.copy(dealt1[1][:].rearrange("p r s t -> p s t r"), picked_str[:, :, :, 2:4])
-        quantize_hubs(dealt0, 0, 0)
         nc.vector.tensor_copy(dealt1[0][:].rearrange("p r s t -> p s t r"), picked_str[:, :, :, 0:2])
+        quantize_hubs(dealt0, 0, 0)
         for c in range(2):
             quantize_hubs(dealt1[c], 1, 2 * c)
 

from contextlib import ExitStack

import concourse.mybir as mybir

D, T, I, Q, J, U, M = 512, 2048, 512, 128, 512, 1024, 2048
FLOPS = 2 * J * D * Q + 2 * Q * J * I

F32 = mybir.dt.float32
BF16 = mybir.dt.bfloat16
I32 = mybir.dt.int32
U32 = mybir.dt.uint32
U16 = mybir.dt.uint16
U8 = mybir.dt.uint8
FP8X4 = mybir.dt.float8_e4m3fn_x4
FP4X4 = mybir.dt.float4_e2m1fn_x4
ALU = mybir.AluOpType
ACT = mybir.ActivationFunctionType

P = 128
PACK = 4
HALF = 256
LIST_COLS = HALF // 16
OUT_EDGES = (0, 256, 768, 1280, 1792, 2048)


def tile_attend_relayed_counts_lean_kernel(
    tc, query, hubs, hf, ties_words, ties_scales, old, fade, offs, offs2, offs3, out
):
    nc = tc.nc
    with ExitStack() as ctx:
        sb = ctx.enter_context(tc.tile_pool(name="sb", bufs=1))
        ps = ctx.enter_context(tc.psum_pool(name="ps", bufs=1))

        def half_of(lst, h):
            return lst[:, h * LIST_COLS : (h + 1) * LIST_COLS]

        tie_list = sb.tile([P, I // 16], U16, name="tie_list")
        hub_list = sb.tile([P, J // 16], U16, name="hub_list")
        col_list = sb.tile([P, I // 16], U16, name="col_list")

        tie_scales = sb.tile([P, T], U8, name="tie_scales", tag="old", align_bytes=64)
        nc.vector.memset(tie_scales[:].bitcast(I32), 0)
        placed = sb.tile([P, M], F32, name="placed")
        nc.vector.memset(placed[:], 0.0)

        nc.sync.dma_start(hub_list[:], offs2)
        hub_rows = hubs.rearrange("(p t) u -> t p u", t=PACK)
        planes = [sb.tile([P, U], F32, name="plane%d" % t) for t in range(PACK)]
        nc.sync.dma_start(planes[0][:], hub_rows[0])
        nc.sync.dma_start(tie_list[:], offs)
        nc.sync.dma_start(tie_scales[0:P:8, :].bitcast(I32), ties_scales[0].bitcast(I32))
        q_raw = sb.tile([P, PACK, Q], F32, name="q_raw", tag="words0", align_bytes=64)
        nc.sync.dma_start(q_raw[:], query.rearrange("(p t) q -> p t q", t=PACK))
        for t in range(1, PACK):
            nc.sync.dma_start(planes[t][:], hub_rows[t])
        tie_words = sb.tile([P, T], U16, name="tie_words", align_bytes=64)
        nc.sync.dma_start(tie_words[:].bitcast(I32), ties_words[0].bitcast(I32))
        hf_sb = sb.tile([P, PACK], F32, name="hf_sb", tag="words1", align_bytes=64)
        nc.sync.dma_start(hf_sb[:], hf.rearrange("(p t) o -> p (t o)", t=PACK))
        nc.sync.dma_start(col_list[:], offs3)
        fade_sb = sb.tile([P, 1], F32, name="fade_sb")
        nc.sync.dma_start(fade_sb[:], fade)

        q_bf = sb.tile([P, Q, PACK], BF16, name="q_bf", align_bytes=64)
        nc.scalar.activation(
            q_bf[:].rearrange("p (c i) t -> p c t i", i=4),
            q_raw[:].rearrange("p t (c i) -> p c t i", i=4),
            ACT.Copy,
        )
        q_codes = sb.tile([P, Q], U32, name="q_codes", align_bytes=64)
        q_scales = sb.tile([P, Q], U8, name="q_scales", align_bytes=64)
        nc.vector.quantize_mx(
            out=q_codes[:].bitcast(FP8X4),
            scales=q_scales[:],
            in_=q_bf[:].rearrange("p q t -> p (q t)"),
        )

        S = HALF // PACK
        dealt0 = sb.tile([P, PACK, S, PACK], BF16, name="dealt0", align_bytes=64)
        picked = sb.tile([P, PACK, HALF], BF16, name="picked", tag="words0", align_bytes=64)
        spread_scales = sb.tile([P, I], U8, name="spread_scales")
        for t in range(PACK):
            nc.vector.tensor_copy(
                dealt0[:].rearrange("p r s t -> p s r t")[:, :, :, t],
                planes[t][:].indirect(half_of(hub_list, 0)),
            )
            nc.scalar.activation(
                picked[:, t, :], planes[t][:].indirect(half_of(hub_list, 1)), ACT.Copy
            )
            if t < 2:
                nc.vector.tensor_copy(
                    spread_scales[:, t * HALF : (t + 1) * HALF],
                    tie_scales[:].indirect(half_of(tie_list, t)),
                )
        slot_scales = sb.tile([P, I], U8, name="slot_scales", align_bytes=64)
        nc.vector.memset(slot_scales[:].bitcast(I32), 0)
        for k in range(4):
            nc.sync.dma_start(
                slot_scales[k:P:32, :].bitcast(I32), spread_scales[8 * k : P : 32, :].bitcast(I32)
            )
        old_sb = sb.tile([P, M], F32, name="old_sb", tag="old", align_bytes=64)
        nc.sync.dma_start(old_sb[:], old)

        hub_codes = sb.tile([P, PACK, P], U32, name="hub_codes", align_bytes=64)
        hub_scales = sb.tile([P, PACK, P], U8, name="hub_scales", align_bytes=64)

        def quantize_hubs(dealt, h, r0):
            for r in range(dealt.shape[1]):
                cols = slice(h * S, (h + 1) * S)
                nc.vector.quantize_mx(
                    out=hub_codes[:, r0 + r, cols].bitcast(FP8X4),
                    scales=hub_scales[:, r0 + r, cols],
                    in_=dealt[:, r, :, :].rearrange("p s t -> p (s t)"),
                )

        dealt1 = [sb.tile([P, 2, S, PACK], BF16, name="dealt1_%d" % c, align_bytes=64) for c in range(2)]
        picked_str = picked[:].rearrange("p t (s r) -> p s t r", r=PACK)
        nc.scalar.copy(dealt1[1][:].rearrange("p r s t -> p s t r"), picked_str[:, :, :, 2:4])
        nc.vector.tensor_copy(dealt1[0][:].rearrange("p r s t -> p s t r"), picked_str[:, :, :, 0:2])
        quantize_hubs(dealt0, 0, 0)
        for c in range(2):
            quantize_hubs(dealt1[c], 1, 2 * c)

        hb = ps.tile([P, PACK, Q], F32, name="hb")
        for r in range(PACK):
            nc.tensor.matmul_mx(
                out=hb[:, r, :],
                lhsT=hub_codes[:, r, :].bitcast(FP8X4),
                lhsT_scale=hub_scales[:, r, :],
                rhs=q_codes[:].bitcast(FP8X4),
                rhs_scale=q_scales[:],
                start=True,
                stop=True,
            )

        QH = Q // 2
        hp_bf = [sb.tile([P, QH, PACK], BF16, name="hp_bf%d" % h, align_bytes=64) for h in range(2)]
        hp_codes = sb.tile([P, Q], U32, name="hp_codes", align_bytes=64)
        hp_scales = sb.tile([P, Q], U8, name="hp_scales", align_bytes=64)
        for h in range(2):
            nc.vector.scalar_tensor_tensor(
                out=hp_bf[h][:],
                in0=hb[:].rearrange("p r q -> p q r")[:, h * QH : (h + 1) * QH, :],
                scalar=0.0,
                in1=hf_sb[:].unsqueeze(1).to_broadcast([P, QH, PACK]),
                op0=ALU.max,
                op1=ALU.mult,
            )
        for h in range(2):
            nc.vector.quantize_mx(
                out=hp_codes[:, h * QH : (h + 1) * QH].bitcast(FP8X4),
                scales=hp_scales[:, h * QH : (h + 1) * QH],
                in_=hp_bf[h][:].rearrange("p q t -> p (q t)"),
            )

        slot_words = [sb.tile([P, HALF], U16, name="slot_words%d" % h, tag="words%d" % h, align_bytes=64) for h in range(2)]
        for h in range(2):
            nc.vector.tensor_copy(slot_words[h][:], tie_words[:].indirect(half_of(tie_list, h)))
        FIRST = 128
        w_first = sb.tile([P, FIRST], F32, name="w_first")
        ws_rest = sb.tile([P, I - FIRST], F32, name="ws_rest")
        for lo, hi in ((0, FIRST), (FIRST, HALF), (HALF, I)):
            h = lo // HALF
            score = ps.tile([P, hi - lo], F32, name="score%d" % lo)
            nc.tensor.matmul_mx(
                out=score[:],
                lhsT=hp_codes[:].bitcast(FP8X4),
                lhsT_scale=hp_scales[:],
                rhs=slot_words[h][:, lo - h * HALF : hi - h * HALF].bitcast(FP4X4),
                rhs_scale=slot_scales[:, lo:hi],
                start=True,
                stop=True,
            )
            if lo == 0:
                nc.scalar.activation(w_first[:], score[:], ACT.Relu)
            else:
                nc.scalar.activation(ws_rest[:, lo - FIRST : hi - FIRST], score[:], ACT.Relu, scale=2.0)
        nc.vector.tensor_tensor(
            placed[:].indirect(col_list[:, : FIRST // 16]), w_first[:], w_first[:], ALU.add
        )
        nc.vector.tensor_copy(placed[:].indirect(col_list[:, FIRST // 16 :]), ws_rest[:])

        for lo, hi in zip(OUT_EDGES[:-1], OUT_EDGES[1:]):
            res = sb.tile([P, hi - lo], F32, name="res%d" % lo)
            nc.vector.scalar_tensor_tensor(
                out=res[:],
                in0=old_sb[:, lo:hi],
                scalar=fade_sb[:],
                in1=placed[:, lo:hi],
                op0=ALU.mult,
                op1=ALU.add,
            )
            nc.sync.dma_start(out[:, lo:hi], res[:])
